import numpy as np
import ml_dtypes


def mxq(x, axis, fmt="e4m3"):
    dtype, down = {"e4m3": (ml_dtypes.float8_e4m3fn, 7), "e5m2": (ml_dtypes.float8_e5m2, 14)}[fmt]
    v = np.moveaxis(np.asarray(x, np.float32).astype(ml_dtypes.bfloat16).astype(np.float64), axis, -1)
    blocks = v.reshape(v.shape[:-1] + (-1, 32))
    amax = np.abs(blocks).max(-1, keepdims=True)
    byte = np.maximum(np.where(amax > 0, np.frexp(amax)[1] - 1 + 127, 0) - down, 1)
    scale = np.exp2(byte - 127.0)
    codes = (blocks / scale).astype(np.float32).astype(dtype).astype(np.float64)
    return np.moveaxis((codes * scale).reshape(v.shape), -1, axis)


WIDE = False


def mx_kscale(k):
    if not WIDE:
        return np.ones(k)
    levels = np.array([10, -10, 5, -5, 0])
    if k % 512:
        return np.exp2(np.random.permutation(np.resize(levels, k // 32))).repeat(32)
    a = np.empty((k // 512, 16))
    for p in range(k // 512):
        a[p, :8] = np.random.permutation(np.resize(levels, 8))
        for g in range(8):
            far = levels[np.abs(levels - a[p, g]) >= 10]
            a[p, g + 8] = far[np.random.randint(len(far))]
    return np.exp2(a.ravel()).repeat(32)


BF16 = ml_dtypes.bfloat16


def bf(x):
    return np.asarray(x, np.float32).astype(BF16)


def f64(x):
    return np.asarray(x).astype(np.float64)


T, S, Z, A = 2048, 2048, 512, 1024


def draw0():
    s = mx_kscale(S)
    t = mx_kscale(T)
    slopes = np.random.standard_normal((T, S)) * s
    recon = np.random.standard_normal((S, Z)) / np.sqrt(S) / s[:, None]
    gain = 1 + 0.1 * np.random.standard_normal(Z)
    frame_weight = (1 + 0.1 * np.random.standard_normal(T)) * t
    commands = np.random.standard_normal((T, A)) / np.sqrt(T) / t[:, None]
    return {"slopes": bf(slopes),
            "recon": bf(recon),
            "gain": bf(gain),
            "frame_weight": bf(frame_weight),
            "commands": bf(commands)}


def core(slopes, recon, gain, frame_weight, commands):
    modes = mxq(f64(slopes), 1, "e4m3") @ mxq(f64(recon), 0, "e4m3")
    h = np.tanh(modes * f64(gain)[None, :]) * f64(frame_weight)[:, None]
    return mxq(h, 0, "e4m3").T @ mxq(f64(commands), 0, "e4m3")


def e4m3fn_bytes(y):
    return np.clip(np.asarray(y, np.float64), -448.0, 448.0).astype(np.float32).astype(ml_dtypes.float8_e4m3fn).view(np.uint8)


def e4m3fn_values(b):
    return np.asarray(b, np.uint8).view(ml_dtypes.float8_e4m3fn).astype(np.float64)


def setup_inputs():
    d = draw0()
    x0 = np.asarray(d['slopes']).astype(np.float64)
    s = (np.max(np.abs(x0), axis=(0,), keepdims=True) / 448.0).astype(np.float32)
    out = {}
    for k, v in d.items():
        if k == 'slopes':
            out['slopes_bytes'] = e4m3fn_bytes(x0 / s.astype(np.float64))
            out['slopes_scale'] = s
        else:
            out[k] = v
    return out


def reference(slopes_bytes, slopes_scale, recon, gain, frame_weight, commands):
    return core(e4m3fn_values(slopes_bytes) * slopes_scale.astype(np.float64), recon, gain, frame_weight, commands)

@@ -1,0 +1,372 @@
+from contextlib import ExitStack
+
+import concourse.mybir as mybir
+from concourse.masks import make_identity
+
+F32 = mybir.dt.float32
+BF16 = mybir.dt.bfloat16
+U32 = mybir.dt.uint32
+U8 = mybir.dt.uint8
+E4M3 = mybir.dt.float8_e4m3fn
+E4M3X4 = mybir.dt.float8_e4m3fn_x4
+ADD = mybir.AluOpType.add
+MULT = mybir.AluOpType.mult
+TANH = mybir.ActivationFunctionType.Tanh
+
+T, S, Z, A = 2048, 2048, 512, 1024
+FLOPS = 2 * T * S * Z + 2 * T * Z * A
+
+P = 128
+PASS = 512
+PASSES = 4
+STEPS = 16
+HALF = S // 2
+UNIT = 256
+
+
+def tile_modal_response_estimate_s7_kernel(
+    tc, slopes_bytes, slopes_scale, recon, gain, frame_weight, commands, out
+):
+    nc = tc.nc
+    bytes_view = slopes_bytes.rearrange("(g p t) s -> g p t s", p=P, t=4)
+    recon_view = recon.rearrange("(g p j) z -> g p j z", p=P, j=4)
+    commands_view = commands.rearrange("(g p j) a -> g p j a", p=P, j=4)
+    scale_row = slopes_scale.rearrange("o k -> (o k)")
+
+    with ExitStack() as ctx:
+        once = ctx.enter_context(tc.tile_pool(name="once", bufs=1))
+        work = ctx.enter_context(tc.tile_pool(name="work", bufs=2))
+        psum = ctx.enter_context(tc.psum_pool(name="psum", bufs=1))
+        ctx.enter_context(tc.manual_schedule())
+
+        byte_tiles = [once.tile([P, 4, S], U8, name="bytes%d" % g) for g in range(4)]
+        scale = once.tile([P, S], F32, name="scale")
+        ident = once.tile([P, P], F32, name="ident")
+        gain_rows = once.tile([P, P], BF16, name="gain_rows")
+        gain_rows32 = once.tile([P, P], F32, name="gain_rows32")
+        gain_cols = once.tile([P, 4], F32, name="gain_cols")
+        weight = once.tile([P, 4, 4], BF16, name="weight")
+        warm = once.tile([P, 1], F32, name="warm")
+
+        recon_codes = once.tile([P, PASSES * Z], U32, name="recon_codes", align_bytes=64)
+        recon_planes = once.tile([P, PASSES * Z], U8, name="recon_planes", align_bytes=64)
+        com_codes = once.tile([P, PASSES * A], U32, name="com_codes", align_bytes=64)
+        com_planes = once.tile([P, PASSES * A], U8, name="com_planes", align_bytes=64)
+        h_codes = once.tile([P, PASSES * Z], U32, name="h_codes", align_bytes=64)
+        h_planes = once.tile([P, PASSES * Z], U8, name="h_planes", align_bytes=64)
+
+        recon_raw = {}
+        com_raw = {}
+        grouped = {}
+        words = {}
+        turned = {}
+        codes = {}
+        acc = {}
+        h_raw = {}
+        h_turned = {}
+        h_grouped = {}
+        resp = {}
+        parts = {}
+
+        def load_bytes(g, t0, t1, c0, c1):
+            nc.sync.dma_start(out=byte_tiles[g][:, t0:t1, c0:c1], in_=bytes_view[g][:, t0:t1, c0:c1])
+
+        def load_scale(half):
+            cols = slice(half * HALF, (half + 1) * HALF)
+            nc.sync.dma_start(out=scale[:, cols], in_=scale_row[cols].partition_broadcast(P))
+
+        def load_recon(g):
+            raw = work.tile([P, 4, Z], BF16, name="recon_raw", bufs=4)
+            nc.sync.dma_start(out=raw[:], in_=recon_view[g])
+            recon_raw[g] = raw
+
+        def load_commands(g):
+            raw = work.tile([P, 4, A], BF16, name="com_raw", bufs=2)
+            nc.sync.dma_start(out=raw[:], in_=commands_view[g])
+            com_raw[g] = raw
+
+        def interleave_recon(g):
+            grp = work.tile([P, 4 * Z], BF16, name="recon_grp", bufs=2, align_bytes=64)
+            nc.scalar.copy(
+                out=grp[:].rearrange("p (z j) -> p z j", j=4),
+                in_=recon_raw[g][:].rearrange("p j z -> p z j"),
+            )
+            grouped["recon", g] = grp
+
+        def quantize_recon(g):
+            nc.vector.quantize_mx(
+                out=recon_codes[:, g * Z : (g + 1) * Z].bitcast(E4M3X4),
+                scales=recon_planes[:, g * Z : (g + 1) * Z],
+                in_=grouped["recon", g][:],
+            )
+
+        def interleave_commands(i, copy):
+            g, n = divmod(i, 2)
+            grp = work.tile([P, 4 * 512], BF16, name="com_grp", bufs=5, align_bytes=64)
+            copy(
+                out=grp[:].rearrange("p (a j) -> p a j", j=4),
+                in_=com_raw[g][:, :, n * 512 : (n + 1) * 512].rearrange("p j a -> p a j"),
+            )
+            grouped["com", i] = grp
+
+        def quantize_commands(i):
+            nc.vector.quantize_mx(
+                out=com_codes[:, i * 512 : (i + 1) * 512].bitcast(E4M3X4),
+                scales=com_planes[:, i * 512 : (i + 1) * 512],
+                in_=grouped["com", i][:],
+            )
+
+        def widen(j):
+            unit, half = divmod(j, 2)
+            g, tp = divmod(unit, 2)
+            for e in range(2):
+                wide = work.tile([P, HALF], BF16, name="wide", bufs=5)
+                cols = slice(half * HALF, (half + 1) * HALF)
+                nc.vector.tensor_tensor(
+                    out=wide[:],
+                    in0=byte_tiles[g][:, 2 * tp + e, cols].bitcast(E4M3),
+                    in1=scale[:, cols],
+                    op=MULT,
+                )
+                words[j, e] = wide
+
+        def turn(j):
+            banks = [psum.tile([P, 2, UNIT], F32, name="turn%d" % b) for b in range(2)]
+            for e in range(2):
+                view = words[j, e][:].bitcast(F32)
+                for b in range(2):
+                    for w in range(2):
+                        nc.tensor.transpose(
+                            banks[b][:, w, e * P : (e + 1) * P],
+                            view[:, 256 * b + w : 256 * (b + 1) : 2],
+                            ident[:],
+                        )
+            turned[j] = banks
+
+        def group(j, copies):
+            grp = work.tile([P, 2 * UNIT * 4], BF16, name="slope_grp", bufs=3, align_bytes=64)
+            view = grp[:].bitcast(F32)
+            for b in range(2):
+                copies[b](
+                    out=view[:, 512 * b : 512 * (b + 1)].rearrange("p (r w) -> p r w", w=2),
+                    in_=turned[j][b][:].rearrange("p w r -> p r w"),
+                )
+            grouped["slopes", j] = grp
+
+        def quantize_slopes(j):
+            unit, half = divmod(j, 2)
+            if half == 0:
+                codes[unit] = (
+                    work.tile([P, PASSES * UNIT], U32, name="slope_codes", bufs=4, align_bytes=64),
+                    work.tile([P, PASSES * UNIT], U8, name="slope_planes", bufs=4, align_bytes=64),
+                )
+            cols = slice(half * 512, (half + 1) * 512)
+            nc.vector.quantize_mx(
+                out=codes[unit][0][:, cols].bitcast(E4M3X4),
+                scales=codes[unit][1][:, cols],
+                in_=grouped["slopes", j][:],
+            )
+
+        def stage1(unit, pair):
+            bank = psum.tile([P, 2, UNIT], F32, name="acc%d" % pair)
+            for c in range(2):
+                for g in range(PASSES):
+                    z0 = g * Z + (2 * pair + c) * P
+                    r0 = g * UNIT
+                    nc.tensor.matmul_mx(
+                        out=bank[:, c, :],
+                        lhsT=recon_codes[:, z0 : z0 + P].bitcast(E4M3X4),
+                        lhsT_scale=recon_planes[:, z0 : z0 + P],
+                        rhs=codes[unit][0][:, r0 : r0 + UNIT].bitcast(E4M3X4),
+                        rhs_scale=codes[unit][1][:, r0 : r0 + UNIT],
+                        start=(g == 0),
+                        stop=(g == PASSES - 1),
+                    )
+            acc[unit, pair] = bank
+
+        def limit(unit, pair):
+            g, tp = divmod(unit, 2)
+            if tp == 0 and pair == 0:
+                h_raw[g] = work.tile([P, 4, PASS], F32, name="h_raw", bufs=2)
+            for c in range(2):
+                zc = 2 * pair + c
+                nc.scalar.activation(
+                    out=h_raw[g][:, zc, tp * UNIT : (tp + 1) * UNIT],
+                    in_=acc[unit, pair][:, c, :],
+                    func=TANH,
+                    scale=gain_cols[:, zc : zc + 1],
+                )
+
+        def turn_h(g, zc):
+            bank = psum.tile([P, PASS], F32, name="hturn%d" % (zc % 2))
+            for t in range(4):
+                nc.tensor.transpose(
+                    bank[:, t * P : (t + 1) * P], h_raw[g][:, zc, t * P : (t + 1) * P], ident[:]
+                )
+            h_turned[g, zc] = bank
+
+        def weigh_h(g, zc):
+            if zc == 0:
+                h_grouped[g] = work.tile([P, 4 * Z], BF16, name="h_grp", bufs=2, align_bytes=64)
+            nc.vector.tensor_tensor(
+                out=h_grouped[g][:, zc * 512 : (zc + 1) * 512].rearrange("p (z t) -> p z t", t=4),
+                in0=h_turned[g, zc][:].rearrange("p (t z) -> p z t", t=4),
+                in1=weight[:, g, :].unsqueeze(1).to_broadcast([P, P, 4]),
+                op=MULT,
+            )
+
+        def quantize_h(g, zc, count):
+            cols = slice(g * Z + zc * P, g * Z + (zc + count) * P)
+            nc.vector.quantize_mx(
+                out=h_codes[:, cols].bitcast(E4M3X4),
+                scales=h_planes[:, cols],
+                in_=h_grouped[g][:, zc * 512 : (zc + count) * 512],
+            )
+
+        def stage2(zc, n, passes, bank_name="", last=PASSES - 1):
+            first = passes[0] if bank_name else -1
+            if bank_name:
+                resp[zc, n] = psum.tile([P, 512], F32, name=bank_name)
+            for g in passes:
+                z0 = g * Z + zc * P
+                a0 = g * A + n * 512
+                nc.tensor.matmul_mx(
+                    out=resp[zc, n][:],
+                    lhsT=h_codes[:, z0 : z0 + P].bitcast(E4M3X4),
+                    lhsT_scale=h_planes[:, z0 : z0 + P],
+                    rhs=com_codes[:, a0 : a0 + 512].bitcast(E4M3X4),
+                    rhs_scale=com_planes[:, a0 : a0 + 512],
+                    start=(g == first),
+                    stop=(g == last),
+                )
+
+        def keep_partial(zc, n):
+            part = once.tile([P, 512], F32, name="part%d" % zc)
+            nc.scalar.copy(out=part[:], in_=resp[zc, n][:])
+            parts[zc, n] = part
+
+        def store(zc, n):
+            res = work.tile([P, 512], F32, name="res", bufs=8)
+            if (zc, n) in parts:
+                nc.vector.tensor_tensor(out=res[:], in0=resp[zc, n][:], in1=parts[zc, n][:], op=ADD)
+            else:
+                nc.scalar.copy(out=res[:], in_=resp[zc, n][:])
+            nc.sync.dma_start(out=out[zc * P : (zc + 1) * P, n * 512 : (n + 1) * 512], in_=res[:])
+
+        scopy = nc.scalar.copy
+        vcopy = nc.vector.tensor_copy
+
+        load_scale(0)
+        load_bytes(0, 0, 1, 0, HALF)
+        load_bytes(0, 1, 2, 0, HALF)
+        load_recon(0)
+        load_scale(1)
+        load_bytes(0, 0, 2, HALF, S)
+        load_recon(1)
+        load_bytes(0, 2, 4, 0, S)
+        load_recon(2)
+        load_recon(3)
+        load_bytes(1, 0, 2, 0, S)
+        load_bytes(1, 2, 4, 0, S)
+        load_commands(0)
+        load_bytes(2, 0, 2, 0, S)
+        load_bytes(2, 2, 4, 0, S)
+        load_commands(1)
+        load_bytes(3, 0, 2, 0, S)
+        load_bytes(3, 2, 4, 0, S)
+
+        nc.gpsimd.memset(warm[:], 0.0)
+        nc.gpsimd.memset(gain_rows[:], 0.0)
+        make_identity(nc, ident[:])
+        nc.gpsimd.dma_start(out=gain_rows[0:4, :], in_=gain.rearrange("(c p) -> c p", p=P))
+        nc.gpsimd.dma_start(out=weight[:], in_=frame_weight.rearrange("(g p t) -> p g t", p=P, t=4))
+        nc.gpsimd.tensor_copy(out=gain_rows32[:], in_=gain_rows[:])
+        nc.scalar.activation(out=warm[:], in_=warm[:], func=TANH)
+
+        stage1_step = {}
+        for k in range(16):
+            stage1_step.setdefault(min(max(k + 3, 5 + k // 2), 15) if k < 14 else 99, []).append(divmod(k, 2))
+        h_step = {}
+        for s, pairs in stage1_step.items():
+            for unit, pair in pairs:
+                if unit % 2 == 1:
+                    h_step.setdefault(s + 1, []).append((unit // 2, pair))
+        com_steps = [4, 5, 7, 8, 10, 11, 14, 15]
+        EARLY0 = {11: [0], 12: [1]}
+        EARLY1 = {12: [0, 1]}
+        EARLYP = {12: [0, 1], 13: [2, 3]}
+
+        for s in range(STEPS):
+            if s >= 1:
+                group(s - 1, (scopy, scopy))
+            for g, pair in h_step.get(s, []):
+                turn_h(g, 2 * pair)
+                turn_h(g, 2 * pair + 1)
+            for unit, pair in stage1_step.get(s, []):
+                stage1(unit, pair)
+                limit(unit, pair)
+            for zc in EARLY0.get(s, []):
+                stage2(zc, 0, (0,), "resp%d" % zc)
+            for zc in EARLY1.get(s, []):
+                stage2(zc, 0, (1,))
+            for zc in EARLYP.get(s, []):
+                stage2(zc, 1, (0, 1), "hturn%d" % (zc % 2), 1)
+                keep_partial(zc, 1)
+            if s < 4:
+                interleave_recon(s)
+            if s in com_steps:
+                interleave_commands(com_steps.index(s), scopy)
+
+            widen(s)
+            turn(s)
+            if s >= 1:
+                quantize_slopes(s - 1)
+            if 1 <= s <= 4:
+                quantize_recon(s - 1)
+            for g, pair in h_step.get(s, []):
+                weigh_h(g, 2 * pair)
+                weigh_h(g, 2 * pair + 1)
+                if pair == 1:
+                    quantize_h(g, 0, 4)
+            if s - 1 in com_steps[:4]:
+                quantize_commands(com_steps.index(s - 1))
+            if s == 2:
+                gain_bank = psum.tile([P, P], F32, name="hturn0")
+                nc.tensor.transpose(gain_bank[:], gain_rows32[:], ident[:])
+                nc.vector.tensor_copy(out=gain_cols[:], in_=gain_bank[:, 0:4])
+            if s == 6:
+                load_commands(2)
+            if s == 9:
+                load_commands(3)
+
+        group(15, (scopy, vcopy))
+        quantize_slopes(15)
+        stage1(7, 0)
+        limit(7, 0)
+        stage1(7, 1)
+        limit(7, 1)
+        for i in range(4, 8):
+            quantize_commands(i)
+        for zc in range(2):
+            stage2(zc, 0, (2,))
+            stage2(zc, 1, (2,), "turn%d" % zc)
+        turn_h(3, 0)
+        turn_h(3, 1)
+        stage2(2, 0, (0, 1, 2), "acc0")
+        stage2(2, 1, (2,), "acc1")
+        for zc in range(4):
+            weigh_h(3, zc)
+            quantize_h(3, zc, 1)
+            if zc < 2:
+                turn_h(3, zc + 2)
+            if zc < 3:
+                for n in range(2):
+                    stage2(zc, n, (3,))
+            else:
+                stage2(3, 0, (0, 1, 2, 3), "hturn0")
+                stage2(3, 1, (2, 3), "hturn1")
+            if zc >= 1:
+                store(zc - 1, 0)
+                store(zc - 1, 1)
+        store(3, 0)
+        store(3, 1)

@@ -31,7 +31,6 @@ def tile_modal_response_estimate_s7_kernel(
     bytes_view = slopes_bytes.rearrange("(g p t) s -> g p t s", p=P, t=4)
     recon_view = recon.rearrange("(g p j) z -> g p j z", p=P, j=4)
     commands_view = commands.rearrange("(g p j) a -> g p j a", p=P, j=4)
-    scale_row = slopes_scale.rearrange("o k -> (o k)")
 
     with ExitStack() as ctx:
         once = ctx.enter_context(tc.tile_pool(name="once", bufs=1))
@@ -39,9 +38,10 @@ def tile_modal_response_estimate_s7_kernel(
         psum = ctx.enter_context(tc.psum_pool(name="psum", bufs=1))
         ctx.enter_context(tc.manual_schedule())
 
-        byte_tiles = [once.tile([P, 4, S], U8, name="bytes%d" % g) for g in range(4)]
         scale = once.tile([P, S], F32, name="scale")
         ident = once.tile([P, P], F32, name="ident")
+        scale_rows = once.tile([P, P], F32, name="scale_rows")
+        scale_cols = once.tile([P, 16], F32, name="scale_cols")
         gain_rows = once.tile([P, P], BF16, name="gain_rows")
         gain_rows32 = once.tile([P, P], F32, name="gain_rows32")
         gain_cols = once.tile([P, 4], F32, name="gain_cols")
@@ -55,6 +55,7 @@ def tile_modal_response_estimate_s7_kernel(
         h_codes = once.tile([P, PASSES * Z], U32, name="h_codes", align_bytes=64)
         h_planes = once.tile([P, PASSES * Z], U8, name="h_planes", align_bytes=64)
 
+        byte_rows = {}
         recon_raw = {}
         com_raw = {}
         grouped = {}
@@ -68,12 +69,35 @@ def tile_modal_response_estimate_s7_kernel(
         resp = {}
         parts = {}
 
-        def load_bytes(g, t0, t1, c0, c1):
-            nc.sync.dma_start(out=byte_tiles[g][:, t0:t1, c0:c1], in_=bytes_view[g][:, t0:t1, c0:c1])
+        def load_bytes(unit, halves, es=(0, 1)):
+            g, tp = divmod(unit, 2)
+            k0 = halves[0] * HALF
+            k1 = k0 + len(halves) * HALF
+            t0 = 2 * tp + es[0]
+            label = "bytes%d_%d_%d" % (unit, halves[0], es[0])
+            codes8 = once.tile([P, len(es), k1 - k0], U8, name=label)
+            nc.sync.dma_start(out=codes8[:], in_=bytes_view[g][:, t0 : t0 + len(es), k0:k1])
+            for i, e in enumerate(es):
+                for half in halves:
+                    byte_rows[unit, half, e] = codes8[:, i, half * HALF - k0 : (half + 1) * HALF - k0]
 
-        def load_scale(half):
-            cols = slice(half * HALF, (half + 1) * HALF)
-            nc.sync.dma_start(out=scale[:, cols], in_=scale_row[cols].partition_broadcast(P))
+        def turn_scale():
+            bank = psum.tile([P, P], F32, name="hturn0")
+            nc.tensor.transpose(bank[:], scale_rows[:], ident[:])
+            nc.vector.tensor_copy(out=scale_cols[:], in_=bank[:, 0:16])
+
+        def spread_scale(half):
+            for b in (2 * half, 2 * half + 1):
+                bank = psum.tile([P, 512], F32, name=("resp0", "resp1", "acc0", "acc1")[b])
+                for i in range(4):
+                    m = 4 * b + i
+                    nc.tensor.transpose(
+                        bank[:, i * P : (i + 1) * P],
+                        scale_cols[:, m : m + 1].to_broadcast([P, P]),
+                        ident[:],
+                    )
+                copy = vcopy if b % 2 else scopy
+                copy(out=scale[:, b * 512 : (b + 1) * 512], in_=bank[:])
 
         def load_recon(g):
             raw = work.tile([P, 4, Z], BF16, name="recon_raw", bufs=4)
@@ -88,8 +112,8 @@ def tile_modal_response_estimate_s7_kernel(
         def interleave_recon(g):
             grp = work.tile([P, 4 * Z], BF16, name="recon_grp", bufs=2, align_bytes=64)
             nc.scalar.copy(
-                out=grp[:].rearrange("p (z j) -> p z j", j=4),
-                in_=recon_raw[g][:].rearrange("p j z -> p z j"),
+                out=grp[:].rearrange("p (c i j) -> p c j i", i=4, j=4),
+                in_=recon_raw[g][:].rearrange("p j (c i) -> p c j i", i=4),
             )
             grouped["recon", g] = grp
 
@@ -100,14 +124,16 @@ def tile_modal_response_estimate_s7_kernel(
                 in_=grouped["recon", g][:],
             )
 
-        def interleave_commands(i, copy):
-            g, n = divmod(i, 2)
-            grp = work.tile([P, 4 * 512], BF16, name="com_grp", bufs=5, align_bytes=64)
+        def interleave_commands(part, copy):
+            i = part // 2
+            if part % 2 == 0:
+                grouped["com", i] = work.tile([P, 4 * 512], BF16, name="com_grp", bufs=4, align_bytes=64)
+            a0 = (part % 4) * 256
+            g0 = (part % 2) * 1024
             copy(
-                out=grp[:].rearrange("p (a j) -> p a j", j=4),
-                in_=com_raw[g][:, :, n * 512 : (n + 1) * 512].rearrange("p j a -> p a j"),
+                out=grouped["com", i][:, g0 : g0 + 1024].rearrange("p (c i j) -> p c j i", i=4, j=4),
+                in_=com_raw[i // 2][:, :, a0 : a0 + 256].rearrange("p j (c i) -> p c j i", i=4),
             )
-            grouped["com", i] = grp
 
         def quantize_commands(i):
             nc.vector.quantize_mx(
@@ -118,30 +144,32 @@ def tile_modal_response_estimate_s7_kernel(
 
         def widen(j):
             unit, half = divmod(j, 2)
-            g, tp = divmod(unit, 2)
+            pieces = 2 if j == 0 else 1
+            width = HALF // pieces
             for e in range(2):
                 wide = work.tile([P, HALF], BF16, name="wide", bufs=5)
-                cols = slice(half * HALF, (half + 1) * HALF)
-                nc.vector.tensor_tensor(
-                    out=wide[:],
-                    in0=byte_tiles[g][:, 2 * tp + e, cols].bitcast(E4M3),
-                    in1=scale[:, cols],
-                    op=MULT,
-                )
                 words[j, e] = wide
+            for i in range(pieces):
+                for e in range(2):
+                    k0 = half * HALF + i * width
+                    nc.vector.tensor_tensor(
+                        out=words[j, e][:, i * width : (i + 1) * width],
+                        in0=byte_rows[unit, half, e][:, i * width : (i + 1) * width].bitcast(E4M3),
+                        in1=scale[:, k0 : k0 + width],
+                        op=MULT,
+                    )
 
-        def turn(j):
-            banks = [psum.tile([P, 2, UNIT], F32, name="turn%d" % b) for b in range(2)]
-            for e in range(2):
-                view = words[j, e][:].bitcast(F32)
-                for b in range(2):
-                    for w in range(2):
-                        nc.tensor.transpose(
-                            banks[b][:, w, e * P : (e + 1) * P],
-                            view[:, 256 * b + w : 256 * (b + 1) : 2],
-                            ident[:],
-                        )
-            turned[j] = banks
+        def turn(j, e):
+            if e == 0:
+                turned[j] = [psum.tile([P, 2, UNIT], F32, name="turn%d" % b) for b in range(2)]
+            view = words[j, e][:].bitcast(F32)
+            for b in range(2):
+                for w in range(2):
+                    nc.tensor.transpose(
+                        turned[j][b][:, w, e * P : (e + 1) * P],
+                        view[:, 256 * b + w : 256 * (b + 1) : 2],
+                        ident[:],
+                    )
 
         def group(j, copies):
             grp = work.tile([P, 2 * UNIT * 4], BF16, name="slope_grp", bufs=3, align_bytes=64)
@@ -167,11 +195,11 @@ def tile_modal_response_estimate_s7_kernel(
                 in_=grouped["slopes", j][:],
             )
 
-        def stage1(unit, pair):
-            bank = psum.tile([P, 2, UNIT], F32, name="acc%d" % pair)
-            for c in range(2):
+        def stage1(unit, zcs, bank_name):
+            bank = psum.tile([P, 2, UNIT], F32, name=bank_name)
+            for c, zc in enumerate(zcs):
                 for g in range(PASSES):
-                    z0 = g * Z + (2 * pair + c) * P
+                    z0 = g * Z + zc * P
                     r0 = g * UNIT
                     nc.tensor.matmul_mx(
                         out=bank[:, c, :],
@@ -182,23 +210,22 @@ def tile_modal_response_estimate_s7_kernel(
                         start=(g == 0),
                         stop=(g == PASSES - 1),
                     )
-            acc[unit, pair] = bank
+                acc[unit, zc] = bank[:, c, :]
 
-        def limit(unit, pair):
+        def limit(unit, zcs):
             g, tp = divmod(unit, 2)
-            if tp == 0 and pair == 0:
+            if unit == 2 * g and zcs[0] == 0:
                 h_raw[g] = work.tile([P, 4, PASS], F32, name="h_raw", bufs=2)
-            for c in range(2):
-                zc = 2 * pair + c
+            for zc in zcs:
                 nc.scalar.activation(
                     out=h_raw[g][:, zc, tp * UNIT : (tp + 1) * UNIT],
-                    in_=acc[unit, pair][:, c, :],
+                    in_=acc[unit, zc],
                     func=TANH,
                     scale=gain_cols[:, zc : zc + 1],
                 )
 
-        def turn_h(g, zc):
-            bank = psum.tile([P, PASS], F32, name="hturn%d" % (zc % 2))
+        def turn_h(g, zc, bank_name):
+            bank = psum.tile([P, PASS], F32, name=bank_name)
             for t in range(4):
                 nc.tensor.transpose(
                     bank[:, t * P : (t + 1) * P], h_raw[g][:, zc, t * P : (t + 1) * P], ident[:]
@@ -241,7 +268,7 @@ def tile_modal_response_estimate_s7_kernel(
                 )
 
         def keep_partial(zc, n):
-            part = once.tile([P, 512], F32, name="part%d" % zc)
+            part = once.tile([P, 512], F32, name="part%d_%d" % (zc, n))
             nc.scalar.copy(out=part[:], in_=resp[zc, n][:])
             parts[zc, n] = part
 
@@ -256,117 +283,123 @@ def tile_modal_response_estimate_s7_kernel(
         scopy = nc.scalar.copy
         vcopy = nc.vector.tensor_copy
 
-        load_scale(0)
-        load_bytes(0, 0, 1, 0, HALF)
-        load_bytes(0, 1, 2, 0, HALF)
+        nc.vector.memset(scale_rows[:], 0.0)
+        nc.vector.memset(gain_rows[:], 0.0)
+        nc.gpsimd.memset(warm[:], 0.0)
+        make_identity(nc, ident[:])
+        nc.sync.dma_start(out=scale_rows[0:16, :], in_=slopes_scale.rearrange("o (m n) -> (o m) n", n=P))
+        load_bytes(0, (0,), (0,))
+        load_bytes(0, (0,), (1,))
+        load_bytes(0, (1,))
         load_recon(0)
-        load_scale(1)
-        load_bytes(0, 0, 2, HALF, S)
         load_recon(1)
-        load_bytes(0, 2, 4, 0, S)
+        load_bytes(1, (0, 1))
         load_recon(2)
         load_recon(3)
-        load_bytes(1, 0, 2, 0, S)
-        load_bytes(1, 2, 4, 0, S)
+        load_bytes(2, (0, 1))
+        load_bytes(3, (0, 1))
         load_commands(0)
-        load_bytes(2, 0, 2, 0, S)
-        load_bytes(2, 2, 4, 0, S)
+        load_bytes(4, (0, 1))
+        load_bytes(5, (0, 1))
         load_commands(1)
-        load_bytes(3, 0, 2, 0, S)
-        load_bytes(3, 2, 4, 0, S)
+        load_bytes(6, (0, 1))
+        load_bytes(7, (0, 1))
 
-        nc.gpsimd.memset(warm[:], 0.0)
-        nc.gpsimd.memset(gain_rows[:], 0.0)
-        make_identity(nc, ident[:])
         nc.gpsimd.dma_start(out=gain_rows[0:4, :], in_=gain.rearrange("(c p) -> c p", p=P))
         nc.gpsimd.dma_start(out=weight[:], in_=frame_weight.rearrange("(g p t) -> p g t", p=P, t=4))
         nc.gpsimd.tensor_copy(out=gain_rows32[:], in_=gain_rows[:])
         nc.scalar.activation(out=warm[:], in_=warm[:], func=TANH)
+        turn_scale()
+        spread_scale(0)
 
         stage1_step = {}
-        for k in range(16):
-            stage1_step.setdefault(min(max(k + 3, 5 + k // 2), 15) if k < 14 else 99, []).append(divmod(k, 2))
+        for k in range(28):
+            stage1_step.setdefault(min(max(k // 2 + 3, 5 + k // 4), 15), []).append(divmod(k, 4))
         h_step = {}
-        for s, pairs in stage1_step.items():
-            for unit, pair in pairs:
+        for s, blocks in stage1_step.items():
+            for unit, zc in blocks:
                 if unit % 2 == 1:
-                    h_step.setdefault(s + 1, []).append((unit // 2, pair))
-        com_steps = [4, 5, 7, 8, 10, 11, 14, 15]
-        EARLY0 = {11: [0], 12: [1]}
-        EARLY1 = {12: [0, 1]}
-        EARLYP = {12: [0, 1], 13: [2, 3]}
+                    h_step.setdefault(s + 1, []).append((unit // 2, zc))
+        com_steps = [4, 5, 5, 7, 7, 7, 8, 9, 10, 11, 11, 13, 14, 15]
+        EARLY = {11: [(0, 0, (0,), "resp0"), (0, 1, (0,), "resp1")], 13: [(0, 0, (1,), ""), (0, 1, (1,), "")]}
+        EARLYP = {12: [(2, 0), (2, 1)], 13: [(3, 0), (3, 1)]}
 
         for s in range(STEPS):
             if s >= 1:
                 group(s - 1, (scopy, scopy))
-            for g, pair in h_step.get(s, []):
-                turn_h(g, 2 * pair)
-                turn_h(g, 2 * pair + 1)
-            for unit, pair in stage1_step.get(s, []):
-                stage1(unit, pair)
-                limit(unit, pair)
-            for zc in EARLY0.get(s, []):
-                stage2(zc, 0, (0,), "resp%d" % zc)
-            for zc in EARLY1.get(s, []):
-                stage2(zc, 0, (1,))
-            for zc in EARLYP.get(s, []):
-                stage2(zc, 1, (0, 1), "hturn%d" % (zc % 2), 1)
-                keep_partial(zc, 1)
+            for g, zc in h_step.get(s, []):
+                turn_h(g, zc, "hturn%d" % (zc % 2))
+            for part, step in enumerate(com_steps):
+                if step == s:
+                    interleave_commands(part, scopy)
+            blocks = stage1_step.get(s, [])
+            mid = len(blocks) // 2
+            for unit, zc in blocks[:mid]:
+                stage1(unit, (zc,), "acc%d" % (zc % 2))
+                limit(unit, (zc,))
+            for zc, n, passes, bank_name in EARLY.get(s, []):
+                stage2(zc, n, passes, bank_name)
+            for zc, n in EARLYP.get(s, []):
+                stage2(zc, n, (0, 1), "hturn%d" % n, 1)
+                keep_partial(zc, n)
             if s < 4:
                 interleave_recon(s)
-            if s in com_steps:
-                interleave_commands(com_steps.index(s), scopy)
 
             widen(s)
-            turn(s)
+            if s == 0:
+                spread_scale(1)
+            turn(s, 0)
+            for unit, zc in blocks[mid:]:
+                stage1(unit, (zc,), "acc%d" % (zc % 2))
+                limit(unit, (zc,))
+            turn(s, 1)
             if s >= 1:
                 quantize_slopes(s - 1)
             if 1 <= s <= 4:
                 quantize_recon(s - 1)
-            for g, pair in h_step.get(s, []):
-                weigh_h(g, 2 * pair)
-                weigh_h(g, 2 * pair + 1)
-                if pair == 1:
+            for g, zc in h_step.get(s, []):
+                weigh_h(g, zc)
+                if zc == 3:
                     quantize_h(g, 0, 4)
-            if s - 1 in com_steps[:4]:
-                quantize_commands(com_steps.index(s - 1))
+            for i in range(6):
+                if com_steps[2 * i + 1] == s - 1:
+                    quantize_commands(i)
             if s == 2:
                 gain_bank = psum.tile([P, P], F32, name="hturn0")
                 nc.tensor.transpose(gain_bank[:], gain_rows32[:], ident[:])
                 nc.vector.tensor_copy(out=gain_cols[:], in_=gain_bank[:, 0:4])
-            if s == 6:
+            if s == com_steps[3]:
                 load_commands(2)
-            if s == 9:
+            if s == com_steps[7]:
                 load_commands(3)
 
         group(15, (scopy, vcopy))
         quantize_slopes(15)
-        stage1(7, 0)
-        limit(7, 0)
-        stage1(7, 1)
-        limit(7, 1)
-        for i in range(4, 8):
-            quantize_commands(i)
-        for zc in range(2):
-            stage2(zc, 0, (2,))
-            stage2(zc, 1, (2,), "turn%d" % zc)
-        turn_h(3, 0)
-        turn_h(3, 1)
-        stage2(2, 0, (0, 1, 2), "acc0")
-        stage2(2, 1, (2,), "acc1")
+        for n in range(2):
+            stage2(0, n, (2,))
+            stage2(1, n, (0, 1, 2), "hturn%d" % n)
         for zc in range(4):
-            weigh_h(3, zc)
-            quantize_h(3, zc, 1)
-            if zc < 2:
-                turn_h(3, zc + 2)
+            stage1(7, (zc,), "acc%d" % (zc % 2))
+            limit(7, (zc,))
+        quantize_commands(6)
+        interleave_commands(14, vcopy)
+        interleave_commands(15, vcopy)
+        quantize_commands(7)
+        for zc in range(4):
+            turn_h(3, zc, ("turn0", "turn1", "acc0", "acc1")[zc])
+        weigh_h(3, 0)
+        for zc in range(4):
             if zc < 3:
+                weigh_h(3, zc + 1)
+            quantize_h(3, zc, 1)
+            if zc == 1:
                 for n in range(2):
+                    stage2(2, n, (2,), "turn%d" % n)
+            for n in range(2):
+                if zc < 3:
                     stage2(zc, n, (3,))
-            else:
-                stage2(3, 0, (0, 1, 2, 3), "hturn0")
-                stage2(3, 1, (2, 3), "hturn1")
-            if zc >= 1:
-                store(zc - 1, 0)
-                store(zc - 1, 1)
-        store(3, 0)
-        store(3, 1)
+                else:
+                    stage2(3, n, (2, 3), "acc%d" % n)
+        for zc in range(4):
+            for n in range(2):
+                store(zc, n)

@@ -86,8 +86,8 @@ def tile_modal_response_estimate_s7_kernel(
             nc.tensor.transpose(bank[:], scale_rows[:], ident[:])
             nc.vector.tensor_copy(out=scale_cols[:], in_=bank[:, 0:16])
 
-        def spread_scale(half):
-            for b in (2 * half, 2 * half + 1):
+        def spread_scale(blocks, copy):
+            for b in blocks:
                 bank = psum.tile([P, 512], F32, name=("resp0", "resp1", "acc0", "acc1")[b])
                 for i in range(4):
                     m = 4 * b + i
@@ -96,7 +96,6 @@ def tile_modal_response_estimate_s7_kernel(
                         scale_cols[:, m : m + 1].to_broadcast([P, P]),
                         ident[:],
                     )
-                copy = vcopy if b % 2 else scopy
                 copy(out=scale[:, b * 512 : (b + 1) * 512], in_=bank[:])
 
         def load_recon(g):
@@ -109,9 +108,9 @@ def tile_modal_response_estimate_s7_kernel(
             nc.sync.dma_start(out=raw[:], in_=commands_view[g])
             com_raw[g] = raw
 
-        def interleave_recon(g):
+        def interleave_recon(g, copy):
             grp = work.tile([P, 4 * Z], BF16, name="recon_grp", bufs=2, align_bytes=64)
-            nc.scalar.copy(
+            copy(
                 out=grp[:].rearrange("p (c i j) -> p c j i", i=4, j=4),
                 in_=recon_raw[g][:].rearrange("p j (c i) -> p c j i", i=4),
             )
@@ -287,11 +286,11 @@ def tile_modal_response_estimate_s7_kernel(
         nc.vector.memset(gain_rows[:], 0.0)
         nc.gpsimd.memset(warm[:], 0.0)
         make_identity(nc, ident[:])
-        nc.sync.dma_start(out=scale_rows[0:16, :], in_=slopes_scale.rearrange("o (m n) -> (o m) n", n=P))
+        load_recon(0)
+        nc.scalar.dma_start(out=scale_rows[0:16, :], in_=slopes_scale.rearrange("o (m n) -> (o m) n", n=P))
         load_bytes(0, (0,), (0,))
         load_bytes(0, (0,), (1,))
         load_bytes(0, (1,))
-        load_recon(0)
         load_recon(1)
         load_bytes(1, (0, 1))
         load_recon(2)
@@ -310,19 +309,20 @@ def tile_modal_response_estimate_s7_kernel(
         nc.gpsimd.tensor_copy(out=gain_rows32[:], in_=gain_rows[:])
         nc.scalar.activation(out=warm[:], in_=warm[:], func=TANH)
         turn_scale()
-        spread_scale(0)
+        interleave_recon(0, vcopy)
+        spread_scale((0, 1, 2), scopy)
 
         stage1_step = {}
         for k in range(28):
-            stage1_step.setdefault(min(max(k // 2 + 3, 5 + k // 4), 15), []).append(divmod(k, 4))
+            stage1_step.setdefault(min(max(k // 2 + 3, 4 + k // 4), 15), []).append(divmod(k, 4))
         h_step = {}
         for s, blocks in stage1_step.items():
             for unit, zc in blocks:
                 if unit % 2 == 1:
                     h_step.setdefault(s + 1, []).append((unit // 2, zc))
-        com_steps = [4, 5, 5, 7, 7, 7, 8, 9, 10, 11, 11, 13, 14, 15]
-        EARLY = {11: [(0, 0, (0,), "resp0"), (0, 1, (0,), "resp1")], 13: [(0, 0, (1,), ""), (0, 1, (1,), "")]}
-        EARLYP = {12: [(2, 0), (2, 1)], 13: [(3, 0), (3, 1)]}
+        com_steps = [3, 3, 4, 5, 6, 7, 7, 7, 9, 11, 11, 13, 14, 15]
+        EARLY = {9: [(0, 0, (0,), "resp0"), (0, 1, (0,), "resp1")], 13: [(0, 0, (1,), ""), (0, 1, (1,), "")]}
+        EARLYP = {12: [(2, 0), (2, 1)], 13: [(3, 0)], 15: [(3, 1)]}
 
         for s in range(STEPS):
             if s >= 1:
@@ -340,14 +340,14 @@ def tile_modal_response_estimate_s7_kernel(
             for zc, n, passes, bank_name in EARLY.get(s, []):
                 stage2(zc, n, passes, bank_name)
             for zc, n in EARLYP.get(s, []):
-                stage2(zc, n, (0, 1), "hturn%d" % n, 1)
+                stage2(zc, n, (0, 1), "hturn%d" % ((zc + n) % 2), 1)
                 keep_partial(zc, n)
-            if s < 4:
-                interleave_recon(s)
+            if s < 3:
+                interleave_recon(s + 1, scopy)
 
             widen(s)
             if s == 0:
-                spread_scale(1)
+                spread_scale((3,), vcopy)
             turn(s, 0)
             for unit, zc in blocks[mid:]:
                 stage1(unit, (zc,), "acc%d" % (zc % 2))
@@ -355,8 +355,8 @@ def tile_modal_response_estimate_s7_kernel(
             turn(s, 1)
             if s >= 1:
                 quantize_slopes(s - 1)
-            if 1 <= s <= 4:
-                quantize_recon(s - 1)
+            if s < 4:
+                quantize_recon(s)
             for g, zc in h_step.get(s, []):
                 weigh_h(g, zc)
                 if zc == 3:
@@ -377,29 +377,35 @@ def tile_modal_response_estimate_s7_kernel(
         quantize_slopes(15)
         for n in range(2):
             stage2(0, n, (2,))
-            stage2(1, n, (0, 1, 2), "hturn%d" % n)
-        for zc in range(4):
+        stage2(1, 0, (0, 1, 2), "hturn0")
+        for zc in range(3):
             stage1(7, (zc,), "acc%d" % (zc % 2))
             limit(7, (zc,))
         quantize_commands(6)
         interleave_commands(14, vcopy)
         interleave_commands(15, vcopy)
         quantize_commands(7)
-        for zc in range(4):
-            turn_h(3, zc, ("turn0", "turn1", "acc0", "acc1")[zc])
+        turn_h(3, 0, "turn0")
+        turn_h(3, 1, "turn1")
+        stage1(7, (3,), "acc1")
+        limit(7, (3,))
+        turn_h(3, 2, "acc0")
         weigh_h(3, 0)
         for zc in range(4):
             if zc < 3:
                 weigh_h(3, zc + 1)
             quantize_h(3, zc, 1)
             if zc == 1:
-                for n in range(2):
-                    stage2(2, n, (2,), "turn%d" % n)
+                stage2(1, 1, (0, 1, 2), "hturn1")
             for n in range(2):
-                if zc < 3:
+                if zc < 2:
                     stage2(zc, n, (3,))
+                elif zc == 2:
+                    stage2(2, n, (2, 3), "turn%d" % n)
                 else:
                     stage2(3, n, (2, 3), "acc%d" % n)
+            if zc == 0:
+                turn_h(3, 3, "acc1")
         for zc in range(4):
             for n in range(2):
                 store(zc, n)

@@ -282,12 +282,12 @@ def tile_modal_response_estimate_s7_kernel(
         scopy = nc.scalar.copy
         vcopy = nc.vector.tensor_copy
 
-        nc.vector.memset(scale_rows[:], 0.0)
+        nc.gpsimd.memset(scale_rows[:], 0.0)
         nc.vector.memset(gain_rows[:], 0.0)
         nc.gpsimd.memset(warm[:], 0.0)
         make_identity(nc, ident[:])
+        nc.sync.dma_start(out=scale_rows[0:16, :], in_=slopes_scale.rearrange("o (m n) -> (o m) n", n=P))
         load_recon(0)
-        nc.scalar.dma_start(out=scale_rows[0:16, :], in_=slopes_scale.rearrange("o (m n) -> (o m) n", n=P))
         load_bytes(0, (0,), (0,))
         load_bytes(0, (0,), (1,))
         load_bytes(0, (1,))
@@ -320,8 +320,8 @@ def tile_modal_response_estimate_s7_kernel(
             for unit, zc in blocks:
                 if unit % 2 == 1:
                     h_step.setdefault(s + 1, []).append((unit // 2, zc))
-        com_steps = [3, 3, 4, 5, 6, 7, 7, 7, 9, 11, 11, 13, 14, 15]
-        EARLY = {9: [(0, 0, (0,), "resp0"), (0, 1, (0,), "resp1")], 13: [(0, 0, (1,), ""), (0, 1, (1,), "")]}
+        com_steps = [3, 3, 4, 5, 7, 7, 7, 8, 9, 10, 11, 12, 14, 15]
+        EARLY = {9: [(0, 0, (0,), "resp0"), (0, 1, (0,), "resp1")], 14: [(0, 0, (1,), ""), (0, 1, (1,), "")]}
         EARLYP = {12: [(2, 0), (2, 1)], 13: [(3, 0)], 15: [(3, 1)]}
 
         for s in range(STEPS):
@@ -353,12 +353,13 @@ def tile_modal_response_estimate_s7_kernel(
                 stage1(unit, (zc,), "acc%d" % (zc % 2))
                 limit(unit, (zc,))
             turn(s, 1)
+            for g, zc in h_step.get(s, []):
+                weigh_h(g, zc)
             if s >= 1:
                 quantize_slopes(s - 1)
             if s < 4:
                 quantize_recon(s)
             for g, zc in h_step.get(s, []):
-                weigh_h(g, zc)
                 if zc == 3:
                     quantize_h(g, 0, 4)
             for i in range(6):
@@ -367,6 +368,7 @@ def tile_modal_response_estimate_s7_kernel(
             if s == 2:
                 gain_bank = psum.tile([P, P], F32, name="hturn0")
                 nc.tensor.transpose(gain_bank[:], gain_rows32[:], ident[:])
+            if s == 3:
                 nc.vector.tensor_copy(out=gain_cols[:], in_=gain_bank[:, 0:4])
             if s == com_steps[3]:
                 load_commands(2)

@@ -17,20 +17,41 @@ T, S, Z, A = 2048, 2048, 512, 1024
 FLOPS = 2 * T * S * Z + 2 * T * Z * A
 
 P = 128
-PASS = 512
-PASSES = 4
-STEPS = 16
+J = 4
+PASSES = S // (P * J)
 HALF = S // 2
-UNIT = 256
+UNIT = 2 * P
+UNITS = T // UNIT
+STEPS = 2 * UNITS
+LAST = UNITS - 1
+MODE_BLOCKS = Z // P
+COLS = 512
+PIECE = 256
+
+COMMAND_STEPS = (3, 3, 5, 6, 6, 7, 8, 8, 9, 9, 10, 11, 12, 13, 14, 15)
+COMMAND_BLOCKS_IN_STEPS = 5
+OPEN_STEPS = {9: 0, 13: 1}
+PARTIAL_STEPS = {12: ((2, 0), (2, 1)), 13: ((3, 0),), 15: ((3, 1),)}
+
+
+def stage1_steps():
+    steps = {}
+    for i in range(LAST * MODE_BLOCKS):
+        step = min(max(i // 2 + 3, i // MODE_BLOCKS + 4), STEPS - 1)
+        steps.setdefault(step, []).append(divmod(i, MODE_BLOCKS))
+    return steps
 
 
 def tile_modal_response_estimate_s7_kernel(
     tc, slopes_bytes, slopes_scale, recon, gain, frame_weight, commands, out
 ):
     nc = tc.nc
-    bytes_view = slopes_bytes.rearrange("(g p t) s -> g p t s", p=P, t=4)
-    recon_view = recon.rearrange("(g p j) z -> g p j z", p=P, j=4)
-    commands_view = commands.rearrange("(g p j) a -> g p j a", p=P, j=4)
+    scalar_copy = nc.scalar.copy
+    vector_copy = nc.vector.tensor_copy
+
+    bytes_view = slopes_bytes.rearrange("(g p t) s -> g p t s", p=P, t=J)
+    recon_view = recon.rearrange("(g p j) z -> g p j z", p=P, j=J)
+    commands_view = commands.rearrange("(g p j) a -> g p j a", p=P, j=J)
 
     with ExitStack() as ctx:
         once = ctx.enter_context(tc.tile_pool(name="once", bufs=1))
@@ -41,373 +62,375 @@ def tile_modal_response_estimate_s7_kernel(
         scale = once.tile([P, S], F32, name="scale")
         ident = once.tile([P, P], F32, name="ident")
         scale_rows = once.tile([P, P], F32, name="scale_rows")
-        scale_cols = once.tile([P, 16], F32, name="scale_cols")
+        scale_cols = once.tile([P, S // P], F32, name="scale_cols")
         gain_rows = once.tile([P, P], BF16, name="gain_rows")
         gain_rows32 = once.tile([P, P], F32, name="gain_rows32")
-        gain_cols = once.tile([P, 4], F32, name="gain_cols")
-        weight = once.tile([P, 4, 4], BF16, name="weight")
+        gain_cols = once.tile([P, MODE_BLOCKS], F32, name="gain_cols")
+        weight = once.tile([P, PASSES, J], BF16, name="weight")
         warm = once.tile([P, 1], F32, name="warm")
 
         recon_codes = once.tile([P, PASSES * Z], U32, name="recon_codes", align_bytes=64)
-        recon_planes = once.tile([P, PASSES * Z], U8, name="recon_planes", align_bytes=64)
+        recon_sbytes = once.tile([P, PASSES * Z], U8, name="recon_sbytes", align_bytes=64)
         com_codes = once.tile([P, PASSES * A], U32, name="com_codes", align_bytes=64)
-        com_planes = once.tile([P, PASSES * A], U8, name="com_planes", align_bytes=64)
+        com_sbytes = once.tile([P, PASSES * A], U8, name="com_sbytes", align_bytes=64)
         h_codes = once.tile([P, PASSES * Z], U32, name="h_codes", align_bytes=64)
-        h_planes = once.tile([P, PASSES * Z], U8, name="h_planes", align_bytes=64)
+        h_sbytes = once.tile([P, PASSES * Z], U8, name="h_sbytes", align_bytes=64)
 
         byte_rows = {}
         recon_raw = {}
+        recon_grouped = {}
         com_raw = {}
-        grouped = {}
-        words = {}
+        com_grouped = {}
+        widened = {}
         turned = {}
-        codes = {}
+        slopes_grouped = {}
+        slope_codes = {}
         acc = {}
         h_raw = {}
         h_turned = {}
         h_grouped = {}
         resp = {}
-        parts = {}
+        partial = {}
 
-        def load_bytes(unit, halves, es=(0, 1)):
-            g, tp = divmod(unit, 2)
+        def load_bytes(unit, halves=(0, 1), rows=(0, 1)):
+            g, pair = divmod(unit, 2)
             k0 = halves[0] * HALF
             k1 = k0 + len(halves) * HALF
-            t0 = 2 * tp + es[0]
-            label = "bytes%d_%d_%d" % (unit, halves[0], es[0])
-            codes8 = once.tile([P, len(es), k1 - k0], U8, name=label)
-            nc.sync.dma_start(out=codes8[:], in_=bytes_view[g][:, t0 : t0 + len(es), k0:k1])
-            for i, e in enumerate(es):
+            t0 = 2 * pair + rows[0]
+            label = "bytes%d_%d_%d" % (unit, halves[0], rows[0])
+            row_bytes = once.tile([P, len(rows), k1 - k0], U8, name=label)
+            nc.sync.dma_start(out=row_bytes[:], in_=bytes_view[g][:, t0 : t0 + len(rows), k0:k1])
+            for i, row in enumerate(rows):
                 for half in halves:
-                    byte_rows[unit, half, e] = codes8[:, i, half * HALF - k0 : (half + 1) * HALF - k0]
-
-        def turn_scale():
-            bank = psum.tile([P, P], F32, name="hturn0")
-            nc.tensor.transpose(bank[:], scale_rows[:], ident[:])
-            nc.vector.tensor_copy(out=scale_cols[:], in_=bank[:, 0:16])
-
-        def spread_scale(blocks, copy):
-            for b in blocks:
-                bank = psum.tile([P, 512], F32, name=("resp0", "resp1", "acc0", "acc1")[b])
-                for i in range(4):
-                    m = 4 * b + i
-                    nc.tensor.transpose(
-                        bank[:, i * P : (i + 1) * P],
-                        scale_cols[:, m : m + 1].to_broadcast([P, P]),
-                        ident[:],
-                    )
-                copy(out=scale[:, b * 512 : (b + 1) * 512], in_=bank[:])
+                    byte_rows[unit, half, row] = row_bytes[:, i, half * HALF - k0 : (half + 1) * HALF - k0]
 
         def load_recon(g):
-            raw = work.tile([P, 4, Z], BF16, name="recon_raw", bufs=4)
+            raw = work.tile([P, J, Z], BF16, name="recon_raw", bufs=4)
             nc.sync.dma_start(out=raw[:], in_=recon_view[g])
             recon_raw[g] = raw
 
         def load_commands(g):
-            raw = work.tile([P, 4, A], BF16, name="com_raw", bufs=2)
+            raw = work.tile([P, J, A], BF16, name="com_raw", bufs=2)
             nc.sync.dma_start(out=raw[:], in_=commands_view[g])
             com_raw[g] = raw
 
-        def interleave_recon(g, copy):
-            grp = work.tile([P, 4 * Z], BF16, name="recon_grp", bufs=2, align_bytes=64)
+        def turn_scales():
+            bank = psum.tile([P, P], F32, name="hturn0")
+            nc.tensor.transpose(bank[:], scale_rows[:], ident[:])
+            nc.vector.tensor_copy(out=scale_cols[:], in_=bank[:, 0 : S // P])
+
+        def spread_scales(bank_index, copy):
+            bank = psum.tile([P, 512], F32, name=("resp0", "resp1", "acc0", "acc1")[bank_index])
+            for i in range(4):
+                m = 4 * bank_index + i
+                nc.tensor.transpose(
+                    bank[:, i * P : (i + 1) * P], scale_cols[:, m : m + 1].to_broadcast([P, P]), ident[:]
+                )
+            copy(out=scale[:, bank_index * 512 : (bank_index + 1) * 512], in_=bank[:])
+
+        def interleave(copy, grouped, raw):
             copy(
-                out=grp[:].rearrange("p (c i j) -> p c j i", i=4, j=4),
-                in_=recon_raw[g][:].rearrange("p j (c i) -> p c j i", i=4),
+                out=grouped.rearrange("p (c i j) -> p c j i", i=4, j=J),
+                in_=raw.rearrange("p j (c i) -> p c j i", i=4),
             )
-            grouped["recon", g] = grp
+
+        def interleave_recon(g, copy):
+            grouped = work.tile([P, J * Z], BF16, name="recon_grouped", bufs=2, align_bytes=64)
+            interleave(copy, grouped[:], recon_raw[g][:])
+            recon_grouped[g] = grouped
 
         def quantize_recon(g):
             nc.vector.quantize_mx(
                 out=recon_codes[:, g * Z : (g + 1) * Z].bitcast(E4M3X4),
-                scales=recon_planes[:, g * Z : (g + 1) * Z],
-                in_=grouped["recon", g][:],
+                scales=recon_sbytes[:, g * Z : (g + 1) * Z],
+                in_=recon_grouped[g][:],
             )
 
-        def interleave_commands(part, copy):
-            i = part // 2
-            if part % 2 == 0:
-                grouped["com", i] = work.tile([P, 4 * 512], BF16, name="com_grp", bufs=4, align_bytes=64)
-            a0 = (part % 4) * 256
-            g0 = (part % 2) * 1024
-            copy(
-                out=grouped["com", i][:, g0 : g0 + 1024].rearrange("p (c i j) -> p c j i", i=4, j=4),
-                in_=com_raw[i // 2][:, :, a0 : a0 + 256].rearrange("p j (c i) -> p c j i", i=4),
+        def interleave_commands(piece):
+            block, part = divmod(piece, 2)
+            if part == 0:
+                com_grouped[block] = work.tile([P, J * COLS], BF16, name="com_grouped", bufs=4, align_bytes=64)
+            a0 = (piece % 4) * PIECE
+            interleave(
+                scalar_copy,
+                com_grouped[block][:, part * J * PIECE : (part + 1) * J * PIECE],
+                com_raw[block // 2][:, :, a0 : a0 + PIECE],
             )
 
-        def quantize_commands(i):
+        def quantize_commands(block):
             nc.vector.quantize_mx(
-                out=com_codes[:, i * 512 : (i + 1) * 512].bitcast(E4M3X4),
-                scales=com_planes[:, i * 512 : (i + 1) * 512],
-                in_=grouped["com", i][:],
+                out=com_codes[:, block * COLS : (block + 1) * COLS].bitcast(E4M3X4),
+                scales=com_sbytes[:, block * COLS : (block + 1) * COLS],
+                in_=com_grouped[block][:],
             )
 
-        def widen(j):
-            unit, half = divmod(j, 2)
-            pieces = 2 if j == 0 else 1
-            width = HALF // pieces
-            for e in range(2):
+        def widen(step):
+            unit, half = divmod(step, 2)
+            for row in range(2):
                 wide = work.tile([P, HALF], BF16, name="wide", bufs=5)
-                words[j, e] = wide
+                widened[step, row] = wide
+            pieces = 2 if step == 0 else 1
+            width = HALF // pieces
             for i in range(pieces):
-                for e in range(2):
+                for row in range(2):
                     k0 = half * HALF + i * width
                     nc.vector.tensor_tensor(
-                        out=words[j, e][:, i * width : (i + 1) * width],
-                        in0=byte_rows[unit, half, e][:, i * width : (i + 1) * width].bitcast(E4M3),
+                        out=widened[step, row][:, i * width : (i + 1) * width],
+                        in0=byte_rows[unit, half, row][:, i * width : (i + 1) * width].bitcast(E4M3),
                         in1=scale[:, k0 : k0 + width],
                         op=MULT,
                     )
 
-        def turn(j, e):
-            if e == 0:
-                turned[j] = [psum.tile([P, 2, UNIT], F32, name="turn%d" % b) for b in range(2)]
-            view = words[j, e][:].bitcast(F32)
+        def turn_slopes(step, row):
+            if row == 0:
+                turned[step] = [psum.tile([P, 2, UNIT], F32, name="turn%d" % b) for b in range(2)]
+            words = widened[step, row][:].bitcast(F32)
             for b in range(2):
                 for w in range(2):
                     nc.tensor.transpose(
-                        turned[j][b][:, w, e * P : (e + 1) * P],
-                        view[:, 256 * b + w : 256 * (b + 1) : 2],
+                        turned[step][b][:, w, row * P : (row + 1) * P],
+                        words[:, 256 * b + w : 256 * (b + 1) : 2],
                         ident[:],
                     )
 
-        def group(j, copies):
-            grp = work.tile([P, 2 * UNIT * 4], BF16, name="slope_grp", bufs=3, align_bytes=64)
-            view = grp[:].bitcast(F32)
+        def group_slopes(step, copies):
+            grouped = work.tile([P, 2 * UNIT * J], BF16, name="slopes_grouped", bufs=3, align_bytes=64)
+            words = grouped[:].bitcast(F32)
             for b in range(2):
                 copies[b](
-                    out=view[:, 512 * b : 512 * (b + 1)].rearrange("p (r w) -> p r w", w=2),
-                    in_=turned[j][b][:].rearrange("p w r -> p r w"),
+                    out=words[:, 512 * b : 512 * (b + 1)].rearrange("p (r w) -> p r w", w=2),
+                    in_=turned[step][b][:].rearrange("p w r -> p r w"),
                 )
-            grouped["slopes", j] = grp
+            slopes_grouped[step] = grouped
 
-        def quantize_slopes(j):
-            unit, half = divmod(j, 2)
+        def quantize_slopes(step):
+            unit, half = divmod(step, 2)
             if half == 0:
-                codes[unit] = (
+                slope_codes[unit] = (
                     work.tile([P, PASSES * UNIT], U32, name="slope_codes", bufs=4, align_bytes=64),
-                    work.tile([P, PASSES * UNIT], U8, name="slope_planes", bufs=4, align_bytes=64),
+                    work.tile([P, PASSES * UNIT], U8, name="slope_sbytes", bufs=4, align_bytes=64),
                 )
-            cols = slice(half * 512, (half + 1) * 512)
+            codes, sbytes = slope_codes[unit]
+            cols = slice(half * 2 * UNIT, (half + 1) * 2 * UNIT)
             nc.vector.quantize_mx(
-                out=codes[unit][0][:, cols].bitcast(E4M3X4),
-                scales=codes[unit][1][:, cols],
-                in_=grouped["slopes", j][:],
+                out=codes[:, cols].bitcast(E4M3X4), scales=sbytes[:, cols], in_=slopes_grouped[step][:]
             )
 
-        def stage1(unit, zcs, bank_name):
+        def stage1(unit, mb, bank_name):
             bank = psum.tile([P, 2, UNIT], F32, name=bank_name)
-            for c, zc in enumerate(zcs):
-                for g in range(PASSES):
-                    z0 = g * Z + zc * P
-                    r0 = g * UNIT
-                    nc.tensor.matmul_mx(
-                        out=bank[:, c, :],
-                        lhsT=recon_codes[:, z0 : z0 + P].bitcast(E4M3X4),
-                        lhsT_scale=recon_planes[:, z0 : z0 + P],
-                        rhs=codes[unit][0][:, r0 : r0 + UNIT].bitcast(E4M3X4),
-                        rhs_scale=codes[unit][1][:, r0 : r0 + UNIT],
-                        start=(g == 0),
-                        stop=(g == PASSES - 1),
-                    )
-                acc[unit, zc] = bank[:, c, :]
-
-        def limit(unit, zcs):
-            g, tp = divmod(unit, 2)
-            if unit == 2 * g and zcs[0] == 0:
-                h_raw[g] = work.tile([P, 4, PASS], F32, name="h_raw", bufs=2)
-            for zc in zcs:
-                nc.scalar.activation(
-                    out=h_raw[g][:, zc, tp * UNIT : (tp + 1) * UNIT],
-                    in_=acc[unit, zc],
-                    func=TANH,
-                    scale=gain_cols[:, zc : zc + 1],
+            codes, sbytes = slope_codes[unit]
+            for g in range(PASSES):
+                z0 = g * Z + mb * P
+                r0 = g * UNIT
+                nc.tensor.matmul_mx(
+                    out=bank[:, 0, :],
+                    lhsT=recon_codes[:, z0 : z0 + P].bitcast(E4M3X4),
+                    lhsT_scale=recon_sbytes[:, z0 : z0 + P],
+                    rhs=codes[:, r0 : r0 + UNIT].bitcast(E4M3X4),
+                    rhs_scale=sbytes[:, r0 : r0 + UNIT],
+                    start=(g == 0),
+                    stop=(g == PASSES - 1),
                 )
+            acc[unit, mb] = bank[:, 0, :]
 
-        def turn_h(g, zc, bank_name):
-            bank = psum.tile([P, PASS], F32, name=bank_name)
-            for t in range(4):
-                nc.tensor.transpose(
-                    bank[:, t * P : (t + 1) * P], h_raw[g][:, zc, t * P : (t + 1) * P], ident[:]
-                )
-            h_turned[g, zc] = bank
+        def limit(unit, mb):
+            g, pair = divmod(unit, 2)
+            if pair == 0 and mb == 0:
+                h_raw[g] = work.tile([P, MODE_BLOCKS, J * P], F32, name="h_raw", bufs=2)
+            nc.scalar.activation(
+                out=h_raw[g][:, mb, pair * UNIT : (pair + 1) * UNIT],
+                in_=acc[unit, mb],
+                func=TANH,
+                scale=gain_cols[:, mb : mb + 1],
+            )
 
-        def weigh_h(g, zc):
-            if zc == 0:
-                h_grouped[g] = work.tile([P, 4 * Z], BF16, name="h_grp", bufs=2, align_bytes=64)
+        def turn_h(g, mb, bank_name):
+            bank = psum.tile([P, J * P], F32, name=bank_name)
+            for t in range(J):
+                nc.tensor.transpose(bank[:, t * P : (t + 1) * P], h_raw[g][:, mb, t * P : (t + 1) * P], ident[:])
+            h_turned[g, mb] = bank
+
+        def weigh_h(g, mb):
+            if mb == 0:
+                h_grouped[g] = work.tile([P, J * Z], BF16, name="h_grouped", bufs=2, align_bytes=64)
             nc.vector.tensor_tensor(
-                out=h_grouped[g][:, zc * 512 : (zc + 1) * 512].rearrange("p (z t) -> p z t", t=4),
-                in0=h_turned[g, zc][:].rearrange("p (t z) -> p z t", t=4),
-                in1=weight[:, g, :].unsqueeze(1).to_broadcast([P, P, 4]),
+                out=h_grouped[g][:, mb * J * P : (mb + 1) * J * P].rearrange("p (z t) -> p z t", t=J),
+                in0=h_turned[g, mb][:].rearrange("p (t z) -> p z t", t=J),
+                in1=weight[:, g, :].unsqueeze(1).to_broadcast([P, P, J]),
                 op=MULT,
             )
 
-        def quantize_h(g, zc, count):
-            cols = slice(g * Z + zc * P, g * Z + (zc + count) * P)
+        def quantize_h(g, mb, count):
+            cols = slice(g * Z + mb * P, g * Z + (mb + count) * P)
             nc.vector.quantize_mx(
                 out=h_codes[:, cols].bitcast(E4M3X4),
-                scales=h_planes[:, cols],
-                in_=h_grouped[g][:, zc * 512 : (zc + count) * 512],
+                scales=h_sbytes[:, cols],
+                in_=h_grouped[g][:, mb * J * P : (mb + count) * J * P],
             )
 
-        def stage2(zc, n, passes, bank_name="", last=PASSES - 1):
-            first = passes[0] if bank_name else -1
+        def stage2(mb, half, groups, bank_name=None, last=PASSES - 1):
             if bank_name:
-                resp[zc, n] = psum.tile([P, 512], F32, name=bank_name)
-            for g in passes:
-                z0 = g * Z + zc * P
-                a0 = g * A + n * 512
+                resp[mb, half] = psum.tile([P, COLS], F32, name=bank_name)
+            for g in groups:
+                z0 = g * Z + mb * P
+                a0 = g * A + half * COLS
                 nc.tensor.matmul_mx(
-                    out=resp[zc, n][:],
+                    out=resp[mb, half][:],
                     lhsT=h_codes[:, z0 : z0 + P].bitcast(E4M3X4),
-                    lhsT_scale=h_planes[:, z0 : z0 + P],
-                    rhs=com_codes[:, a0 : a0 + 512].bitcast(E4M3X4),
-                    rhs_scale=com_planes[:, a0 : a0 + 512],
-                    start=(g == first),
+                    lhsT_scale=h_sbytes[:, z0 : z0 + P],
+                    rhs=com_codes[:, a0 : a0 + COLS].bitcast(E4M3X4),
+                    rhs_scale=com_sbytes[:, a0 : a0 + COLS],
+                    start=(bank_name is not None and g == groups[0]),
                     stop=(g == last),
                 )
 
-        def keep_partial(zc, n):
-            part = once.tile([P, 512], F32, name="part%d_%d" % (zc, n))
-            nc.scalar.copy(out=part[:], in_=resp[zc, n][:])
-            parts[zc, n] = part
+        def keep_partial(mb, half):
+            part = once.tile([P, COLS], F32, name="partial%d_%d" % (mb, half))
+            nc.scalar.copy(out=part[:], in_=resp[mb, half][:])
+            partial[mb, half] = part
 
-        def store(zc, n):
-            res = work.tile([P, 512], F32, name="res", bufs=8)
-            if (zc, n) in parts:
-                nc.vector.tensor_tensor(out=res[:], in0=resp[zc, n][:], in1=parts[zc, n][:], op=ADD)
+        def store(mb, half):
+            result = work.tile([P, COLS], F32, name="result", bufs=8)
+            if (mb, half) in partial:
+                nc.vector.tensor_tensor(
+                    out=result[:], in0=resp[mb, half][:], in1=partial[mb, half][:], op=ADD
+                )
             else:
-                nc.scalar.copy(out=res[:], in_=resp[zc, n][:])
-            nc.sync.dma_start(out=out[zc * P : (zc + 1) * P, n * 512 : (n + 1) * 512], in_=res[:])
-
-        scopy = nc.scalar.copy
-        vcopy = nc.vector.tensor_copy
+                nc.scalar.copy(out=result[:], in_=resp[mb, half][:])
+            nc.sync.dma_start(
+                out=out[mb * P : (mb + 1) * P, half * COLS : (half + 1) * COLS], in_=result[:]
+            )
 
         nc.gpsimd.memset(scale_rows[:], 0.0)
         nc.vector.memset(gain_rows[:], 0.0)
         nc.gpsimd.memset(warm[:], 0.0)
         make_identity(nc, ident[:])
-        nc.sync.dma_start(out=scale_rows[0:16, :], in_=slopes_scale.rearrange("o (m n) -> (o m) n", n=P))
+        nc.sync.dma_start(out=scale_rows[0 : S // P, :], in_=slopes_scale.rearrange("o (m n) -> (o m) n", n=P))
         load_recon(0)
+        nc.sync.dma_start(out=gain_rows[0:MODE_BLOCKS, :], in_=gain.rearrange("(c p) -> c p", p=P))
         load_bytes(0, (0,), (0,))
         load_bytes(0, (0,), (1,))
         load_bytes(0, (1,))
         load_recon(1)
-        load_bytes(1, (0, 1))
+        load_bytes(1)
         load_recon(2)
         load_recon(3)
-        load_bytes(2, (0, 1))
-        load_bytes(3, (0, 1))
+        nc.sync.dma_start(out=weight[:], in_=frame_weight.rearrange("(g p t) -> p g t", p=P, t=J))
+        load_bytes(2)
+        load_bytes(3)
         load_commands(0)
-        load_bytes(4, (0, 1))
-        load_bytes(5, (0, 1))
+        load_bytes(4)
+        load_bytes(5)
         load_commands(1)
-        load_bytes(6, (0, 1))
-        load_bytes(7, (0, 1))
+        load_bytes(6)
+        load_bytes(7)
 
-        nc.gpsimd.dma_start(out=gain_rows[0:4, :], in_=gain.rearrange("(c p) -> c p", p=P))
-        nc.gpsimd.dma_start(out=weight[:], in_=frame_weight.rearrange("(g p t) -> p g t", p=P, t=4))
-        nc.gpsimd.tensor_copy(out=gain_rows32[:], in_=gain_rows[:])
         nc.scalar.activation(out=warm[:], in_=warm[:], func=TANH)
-        turn_scale()
-        interleave_recon(0, vcopy)
-        spread_scale((0, 1, 2), scopy)
+        turn_scales()
+        interleave_recon(0, vector_copy)
+        for bank_index in range(3):
+            spread_scales(bank_index, scalar_copy)
+        nc.scalar.copy(out=gain_rows32[:], in_=gain_rows[:])
 
-        stage1_step = {}
-        for k in range(28):
-            stage1_step.setdefault(min(max(k // 2 + 3, 4 + k // 4), 15), []).append(divmod(k, 4))
-        h_step = {}
-        for s, blocks in stage1_step.items():
-            for unit, zc in blocks:
+        stage1_blocks = stage1_steps()
+        h_blocks = {}
+        for step, blocks in stage1_blocks.items():
+            for unit, mb in blocks:
                 if unit % 2 == 1:
-                    h_step.setdefault(s + 1, []).append((unit // 2, zc))
-        com_steps = [3, 3, 4, 5, 7, 7, 7, 8, 9, 10, 11, 12, 14, 15]
-        EARLY = {9: [(0, 0, (0,), "resp0"), (0, 1, (0,), "resp1")], 14: [(0, 0, (1,), ""), (0, 1, (1,), "")]}
-        EARLYP = {12: [(2, 0), (2, 1)], 13: [(3, 0)], 15: [(3, 1)]}
+                    h_blocks.setdefault(step + 1, []).append((unit // 2, mb))
 
-        for s in range(STEPS):
-            if s >= 1:
-                group(s - 1, (scopy, scopy))
-            for g, zc in h_step.get(s, []):
-                turn_h(g, zc, "hturn%d" % (zc % 2))
-            for part, step in enumerate(com_steps):
-                if step == s:
-                    interleave_commands(part, scopy)
-            blocks = stage1_step.get(s, [])
-            mid = len(blocks) // 2
-            for unit, zc in blocks[:mid]:
-                stage1(unit, (zc,), "acc%d" % (zc % 2))
-                limit(unit, (zc,))
-            for zc, n, passes, bank_name in EARLY.get(s, []):
-                stage2(zc, n, passes, bank_name)
-            for zc, n in EARLYP.get(s, []):
-                stage2(zc, n, (0, 1), "hturn%d" % ((zc + n) % 2), 1)
-                keep_partial(zc, n)
-            if s < 3:
-                interleave_recon(s + 1, scopy)
+        for step in range(STEPS):
+            if step >= 1:
+                group_slopes(step - 1, (scalar_copy, scalar_copy))
+            for g, mb in h_blocks.get(step, []):
+                turn_h(g, mb, "hturn%d" % (mb % 2))
+            for piece, piece_step in enumerate(COMMAND_STEPS):
+                if piece_step == step:
+                    interleave_commands(piece)
 
-            widen(s)
-            if s == 0:
-                spread_scale((3,), vcopy)
-            turn(s, 0)
-            for unit, zc in blocks[mid:]:
-                stage1(unit, (zc,), "acc%d" % (zc % 2))
-                limit(unit, (zc,))
-            turn(s, 1)
-            for g, zc in h_step.get(s, []):
-                weigh_h(g, zc)
-            if s >= 1:
-                quantize_slopes(s - 1)
-            if s < 4:
-                quantize_recon(s)
-            for g, zc in h_step.get(s, []):
-                if zc == 3:
-                    quantize_h(g, 0, 4)
-            for i in range(6):
-                if com_steps[2 * i + 1] == s - 1:
-                    quantize_commands(i)
-            if s == 2:
+            blocks = stage1_blocks.get(step, [])
+            before = len(blocks) // 2
+            for unit, mb in blocks[:before]:
+                stage1(unit, mb, "acc%d" % (mb % 2))
+                limit(unit, mb)
+            if step in OPEN_STEPS:
+                g = OPEN_STEPS[step]
+                for half in range(2):
+                    stage2(0, half, (g,), "resp%d" % half if g == 0 else None)
+            for mb, half in PARTIAL_STEPS.get(step, ()):
+                stage2(mb, half, (0, 1), "hturn%d" % ((mb + half) % 2), last=1)
+                keep_partial(mb, half)
+            if step < PASSES - 1:
+                interleave_recon(step + 1, scalar_copy)
+
+            widen(step)
+            if step == 0:
+                spread_scales(3, vector_copy)
+            turn_slopes(step, 0)
+            for unit, mb in blocks[before:]:
+                stage1(unit, mb, "acc%d" % (mb % 2))
+                limit(unit, mb)
+            turn_slopes(step, 1)
+
+            for g, mb in h_blocks.get(step, []):
+                weigh_h(g, mb)
+            if step >= 1:
+                quantize_slopes(step - 1)
+            if step < PASSES:
+                quantize_recon(step)
+            for block in range(COMMAND_BLOCKS_IN_STEPS):
+                if COMMAND_STEPS[2 * block + 1] == step - 1:
+                    quantize_commands(block)
+            for g, mb in h_blocks.get(step, []):
+                if mb == MODE_BLOCKS - 1:
+                    quantize_h(g, 0, MODE_BLOCKS)
+
+            if step == 2:
                 gain_bank = psum.tile([P, P], F32, name="hturn0")
                 nc.tensor.transpose(gain_bank[:], gain_rows32[:], ident[:])
-            if s == 3:
-                nc.vector.tensor_copy(out=gain_cols[:], in_=gain_bank[:, 0:4])
-            if s == com_steps[3]:
-                load_commands(2)
-            if s == com_steps[7]:
-                load_commands(3)
+            if step == 3:
+                nc.vector.tensor_copy(out=gain_cols[:], in_=gain_bank[:, 0:MODE_BLOCKS])
+            for g in (0, 1):
+                if step == COMMAND_STEPS[4 * g + 3]:
+                    load_commands(g + 2)
 
-        group(15, (scopy, vcopy))
-        quantize_slopes(15)
-        for n in range(2):
-            stage2(0, n, (2,))
+        group_slopes(STEPS - 1, (scalar_copy, vector_copy))
+        quantize_slopes(STEPS - 1)
+        stage2(0, 0, (2,))
         stage2(1, 0, (0, 1, 2), "hturn0")
-        for zc in range(3):
-            stage1(7, (zc,), "acc%d" % (zc % 2))
-            limit(7, (zc,))
-        quantize_commands(6)
-        interleave_commands(14, vcopy)
-        interleave_commands(15, vcopy)
-        quantize_commands(7)
+        for mb in range(3):
+            stage1(LAST, mb, "acc%d" % (mb % 2))
+            limit(LAST, mb)
+        for block in (6, 5, 7):
+            quantize_commands(block)
         turn_h(3, 0, "turn0")
         turn_h(3, 1, "turn1")
-        stage1(7, (3,), "acc1")
-        limit(7, (3,))
+        stage1(LAST, 3, "acc1")
+        limit(LAST, 3)
         turn_h(3, 2, "acc0")
         weigh_h(3, 0)
-        for zc in range(4):
-            if zc < 3:
-                weigh_h(3, zc + 1)
-            quantize_h(3, zc, 1)
-            if zc == 1:
-                stage2(1, 1, (0, 1, 2), "hturn1")
-            for n in range(2):
-                if zc < 2:
-                    stage2(zc, n, (3,))
-                elif zc == 2:
-                    stage2(2, n, (2, 3), "turn%d" % n)
-                else:
-                    stage2(3, n, (2, 3), "acc%d" % n)
-            if zc == 0:
-                turn_h(3, 3, "acc1")
-        for zc in range(4):
-            for n in range(2):
-                store(zc, n)
+
+        weigh_h(3, 1)
+        quantize_h(3, 0, 1)
+        stage2(0, 0, (3,))
+        stage2(0, 1, (2, 3))
+        turn_h(3, 3, "acc1")
+
+        weigh_h(3, 2)
+        quantize_h(3, 1, 1)
+        stage2(1, 1, (0, 1, 2), "hturn1")
+        for half in range(2):
+            stage2(1, half, (3,))
+
+        weigh_h(3, 3)
+        quantize_h(3, 2, 1)
+        for half in range(2):
+            stage2(2, half, (2, 3), "turn%d" % half)
+
+        quantize_h(3, 3, 1)
+        for half in range(2):
+            stage2(3, half, (2, 3), "acc%d" % half)
+
+        for mb in range(MODE_BLOCKS):
+            for half in range(2):
+                store(mb, half)

from contextlib import ExitStack

import concourse.mybir as mybir
from concourse.masks import make_identity

F32 = mybir.dt.float32
BF16 = mybir.dt.bfloat16
U32 = mybir.dt.uint32
U8 = mybir.dt.uint8
E4M3 = mybir.dt.float8_e4m3fn
E4M3X4 = mybir.dt.float8_e4m3fn_x4
ADD = mybir.AluOpType.add
MULT = mybir.AluOpType.mult
TANH = mybir.ActivationFunctionType.Tanh

T, S, Z, A = 2048, 2048, 512, 1024
FLOPS = 2 * T * S * Z + 2 * T * Z * A

P = 128
J = 4
PASSES = S // (P * J)
HALF = S // 2
UNIT = 2 * P
UNITS = T // UNIT
STEPS = 2 * UNITS
LAST = UNITS - 1
MODE_BLOCKS = Z // P
COLS = 512
PIECE = 256

COMMAND_STEPS = (3, 3, 5, 6, 6, 7, 8, 8, 9, 9, 10, 11, 12, 13, 14, 15)
COMMAND_BLOCKS_IN_STEPS = 5
OPEN_STEPS = {9: 0, 13: 1}
PARTIAL_STEPS = {12: ((2, 0), (2, 1)), 13: ((3, 0),), 15: ((3, 1),)}


def stage1_steps():
    steps = {}
    for i in range(LAST * MODE_BLOCKS):
        step = min(max(i // 2 + 3, i // MODE_BLOCKS + 4), STEPS - 1)
        steps.setdefault(step, []).append(divmod(i, MODE_BLOCKS))
    return steps


def tile_modal_response_estimate_s7_kernel(
    tc, slopes_bytes, slopes_scale, recon, gain, frame_weight, commands, out
):
    nc = tc.nc
    scalar_copy = nc.scalar.copy
    vector_copy = nc.vector.tensor_copy

    bytes_view = slopes_bytes.rearrange("(g p t) s -> g p t s", p=P, t=J)
    recon_view = recon.rearrange("(g p j) z -> g p j z", p=P, j=J)
    commands_view = commands.rearrange("(g p j) a -> g p j a", p=P, j=J)

    with ExitStack() as ctx:
        once = ctx.enter_context(tc.tile_pool(name="once", bufs=1))
        work = ctx.enter_context(tc.tile_pool(name="work", bufs=2))
        psum = ctx.enter_context(tc.psum_pool(name="psum", bufs=1))
        ctx.enter_context(tc.manual_schedule())

        scale = once.tile([P, S], F32, name="scale")
        ident = once.tile([P, P], F32, name="ident")
        scale_rows = once.tile([P, P], F32, name="scale_rows")
        scale_cols = once.tile([P, S // P], F32, name="scale_cols")
        gain_rows = once.tile([P, P], BF16, name="gain_rows")
        gain_rows32 = once.tile([P, P], F32, name="gain_rows32")
        gain_cols = once.tile([P, MODE_BLOCKS], F32, name="gain_cols")
        weight = once.tile([P, PASSES, J], BF16, name="weight")
        warm = once.tile([P, 1], F32, name="warm")

        recon_codes = once.tile([P, PASSES * Z], U32, name="recon_codes", align_bytes=64)
        recon_sbytes = once.tile([P, PASSES * Z], U8, name="recon_sbytes", align_bytes=64)
        com_codes = once.tile([P, PASSES * A], U32, name="com_codes", align_bytes=64)
        com_sbytes = once.tile([P, PASSES * A], U8, name="com_sbytes", align_bytes=64)
        h_codes = once.tile([P, PASSES * Z], U32, name="h_codes", align_bytes=64)
        h_sbytes = once.tile([P, PASSES * Z], U8, name="h_sbytes", align_bytes=64)

        byte_rows = {}
        recon_raw = {}
        recon_grouped = {}
        com_raw = {}
        com_grouped = {}
        widened = {}
        turned = {}
        slopes_grouped = {}
        slope_codes = {}
        acc = {}
        h_raw = {}
        h_turned = {}
        h_grouped = {}
        resp = {}
        partial = {}

        def load_bytes(unit, halves=(0, 1), rows=(0, 1)):
            g, pair = divmod(unit, 2)
            k0 = halves[0] * HALF
            k1 = k0 + len(halves) * HALF
            t0 = 2 * pair + rows[0]
            label = "bytes%d_%d_%d" % (unit, halves[0], rows[0])
            row_bytes = once.tile([P, len(rows), k1 - k0], U8, name=label)
            nc.sync.dma_start(out=row_bytes[:], in_=bytes_view[g][:, t0 : t0 + len(rows), k0:k1])
            for i, row in enumerate(rows):
                for half in halves:
                    byte_rows[unit, half, row] = row_bytes[:, i, half * HALF - k0 : (half + 1) * HALF - k0]

        def load_recon(g):
            raw = work.tile([P, J, Z], BF16, name="recon_raw", bufs=4)
            nc.sync.dma_start(out=raw[:], in_=recon_view[g])
            recon_raw[g] = raw

        def load_commands(g):
            raw = work.tile([P, J, A], BF16, name="com_raw", bufs=2)
            nc.sync.dma_start(out=raw[:], in_=commands_view[g])
            com_raw[g] = raw

        def turn_scales():
            bank = psum.tile([P, P], F32, name="hturn0")
            nc.tensor.transpose(bank[:], scale_rows[:], ident[:])
            nc.vector.tensor_copy(out=scale_cols[:], in_=bank[:, 0 : S // P])

        def spread_scales(bank_index, copy):
            bank = psum.tile([P, 512], F32, name=("resp0", "resp1", "acc0", "acc1")[bank_index])
            for i in range(4):
                m = 4 * bank_index + i
                nc.tensor.transpose(
                    bank[:, i * P : (i + 1) * P], scale_cols[:, m : m + 1].to_broadcast([P, P]), ident[:]
                )
            copy(out=scale[:, bank_index * 512 : (bank_index + 1) * 512], in_=bank[:])

        def interleave(copy, grouped, raw):
            copy(
                out=grouped.rearrange("p (c i j) -> p c j i", i=4, j=J),
                in_=raw.rearrange("p j (c i) -> p c j i", i=4),
            )

        def interleave_recon(g, copy):
            grouped = work.tile([P, J * Z], BF16, name="recon_grouped", bufs=2, align_bytes=64)
            interleave(copy, grouped[:], recon_raw[g][:])
            recon_grouped[g] = grouped

        def quantize_recon(g):
            nc.vector.quantize_mx(
                out=recon_codes[:, g * Z : (g + 1) * Z].bitcast(E4M3X4),
                scales=recon_sbytes[:, g * Z : (g + 1) * Z],
                in_=recon_grouped[g][:],
            )

        def interleave_commands(piece):
            block, part = divmod(piece, 2)
            if part == 0:
                com_grouped[block] = work.tile([P, J * COLS], BF16, name="com_grouped", bufs=4, align_bytes=64)
            a0 = (piece % 4) * PIECE
            interleave(
                scalar_copy,
                com_grouped[block][:, part * J * PIECE : (part + 1) * J * PIECE],
                com_raw[block // 2][:, :, a0 : a0 + PIECE],
            )

        def quantize_commands(block):
            nc.vector.quantize_mx(
                out=com_codes[:, block * COLS : (block + 1) * COLS].bitcast(E4M3X4),
                scales=com_sbytes[:, block * COLS : (block + 1) * COLS],
                in_=com_grouped[block][:],
            )

        def widen(step):
            unit, half = divmod(step, 2)
            for row in range(2):
                wide = work.tile([P, HALF], BF16, name="wide", bufs=5)
                widened[step, row] = wide
            pieces = 2 if step == 0 else 1
            width = HALF // pieces
            for i in range(pieces):
                for row in range(2):
                    k0 = half * HALF + i * width
                    nc.vector.tensor_tensor(
                        out=widened[step, row][:, i * width : (i + 1) * width],
                        in0=byte_rows[unit, half, row][:, i * width : (i + 1) * width].bitcast(E4M3),
                        in1=scale[:, k0 : k0 + width],
                        op=MULT,
                    )

        def turn_slopes(step, row):
            if row == 0:
                turned[step] = [psum.tile([P, 2, UNIT], F32, name="turn%d" % b) for b in range(2)]
            words = widened[step, row][:].bitcast(F32)
            for b in range(2):
                for w in range(2):
                    nc.tensor.transpose(
                        turned[step][b][:, w, row * P : (row + 1) * P],
                        words[:, 256 * b + w : 256 * (b + 1) : 2],
                        ident[:],
                    )

        def group_slopes(step, copies):
            grouped = work.tile([P, 2 * UNIT * J], BF16, name="slopes_grouped", bufs=3, align_bytes=64)
            words = grouped[:].bitcast(F32)
            for b in range(2):
                copies[b](
                    out=words[:, 512 * b : 512 * (b + 1)].rearrange("p (r w) -> p r w", w=2),
                    in_=turned[step][b][:].rearrange("p w r -> p r w"),
                )
            slopes_grouped[step] = grouped

        def quantize_slopes(step):
            unit, half = divmod(step, 2)
            if half == 0:
                slope_codes[unit] = (
                    work.tile([P, PASSES * UNIT], U32, name="slope_codes", bufs=4, align_bytes=64),
                    work.tile([P, PASSES * UNIT], U8, name="slope_sbytes", bufs=4, align_bytes=64),
                )
            codes, sbytes = slope_codes[unit]
            cols = slice(half * 2 * UNIT, (half + 1) * 2 * UNIT)
            nc.vector.quantize_mx(
                out=codes[:, cols].bitcast(E4M3X4), scales=sbytes[:, cols], in_=slopes_grouped[step][:]
            )

        def stage1(unit, mb, bank_name):
            bank = psum.tile([P, 2, UNIT], F32, name=bank_name)
            codes, sbytes = slope_codes[unit]
            for g in range(PASSES):
                z0 = g * Z + mb * P
                r0 = g * UNIT
                nc.tensor.matmul_mx(
                    out=bank[:, 0, :],
                    lhsT=recon_codes[:, z0 : z0 + P].bitcast(E4M3X4),
                    lhsT_scale=recon_sbytes[:, z0 : z0 + P],
                    rhs=codes[:, r0 : r0 + UNIT].bitcast(E4M3X4),
                    rhs_scale=sbytes[:, r0 : r0 + UNIT],
                    start=(g == 0),
                    stop=(g == PASSES - 1),
                )
            acc[unit, mb] = bank[:, 0, :]

        def limit(unit, mb):
            g, pair = divmod(unit, 2)
            if pair == 0 and mb == 0:
                h_raw[g] = work.tile([P, MODE_BLOCKS, J * P], F32, name="h_raw", bufs=2)
            nc.scalar.activation(
                out=h_raw[g][:, mb, pair * UNIT : (pair + 1) * UNIT],
                in_=acc[unit, mb],
                func=TANH,
                scale=gain_cols[:, mb : mb + 1],
            )

        def turn_h(g, mb, bank_name):
            bank = psum.tile([P, J * P], F32, name=bank_name)
            for t in range(J):
                nc.tensor.transpose(bank[:, t * P : (t + 1) * P], h_raw[g][:, mb, t * P : (t + 1) * P], ident[:])
            h_turned[g, mb] = bank

        def weigh_h(g, mb):
            if mb == 0:
                h_grouped[g] = work.tile([P, J * Z], BF16, name="h_grouped", bufs=2, align_bytes=64)
            nc.vector.tensor_tensor(
                out=h_grouped[g][:, mb * J * P : (mb + 1) * J * P].rearrange("p (z t) -> p z t", t=J),
                in0=h_turned[g, mb][:].rearrange("p (t z) -> p z t", t=J),
                in1=weight[:, g, :].unsqueeze(1).to_broadcast([P, P, J]),
                op=MULT,
            )

        def quantize_h(g, mb, count):
            cols = slice(g * Z + mb * P, g * Z + (mb + count) * P)
            nc.vector.quantize_mx(
                out=h_codes[:, cols].bitcast(E4M3X4),
                scales=h_sbytes[:, cols],
                in_=h_grouped[g][:, mb * J * P : (mb + count) * J * P],
            )

        def stage2(mb, half, groups, bank_name=None, last=PASSES - 1):
            if bank_name:
                resp[mb, half] = psum.tile([P, COLS], F32, name=bank_name)
            for g in groups:
                z0 = g * Z + mb * P
                a0 = g * A + half * COLS
                nc.tensor.matmul_mx(
                    out=resp[mb, half][:],
                    lhsT=h_codes[:, z0 : z0 + P].bitcast(E4M3X4),
                    lhsT_scale=h_sbytes[:, z0 : z0 + P],
                    rhs=com_codes[:, a0 : a0 + COLS].bitcast(E4M3X4),
                    rhs_scale=com_sbytes[:, a0 : a0 + COLS],
                    start=(bank_name is not None and g == groups[0]),
                    stop=(g == last),
                )

        def keep_partial(mb, half):
            part = once.tile([P, COLS], F32, name="partial%d_%d" % (mb, half))
            nc.scalar.copy(out=part[:], in_=resp[mb, half][:])
            partial[mb, half] = part

        def store(mb, half):
            result = work.tile([P, COLS], F32, name="result", bufs=8)
            if (mb, half) in partial:
                nc.vector.tensor_tensor(
                    out=result[:], in0=resp[mb, half][:], in1=partial[mb, half][:], op=ADD
                )
            else:
                nc.scalar.copy(out=result[:], in_=resp[mb, half][:])
            nc.sync.dma_start(
                out=out[mb * P : (mb + 1) * P, half * COLS : (half + 1) * COLS], in_=result[:]
            )

        nc.gpsimd.memset(scale_rows[:], 0.0)
        nc.vector.memset(gain_rows[:], 0.0)
        nc.gpsimd.memset(warm[:], 0.0)
        make_identity(nc, ident[:])
        nc.sync.dma_start(out=scale_rows[0 : S // P, :], in_=slopes_scale.rearrange("o (m n) -> (o m) n", n=P))
        load_recon(0)
        nc.sync.dma_start(out=gain_rows[0:MODE_BLOCKS, :], in_=gain.rearrange("(c p) -> c p", p=P))
        load_bytes(0, (0,), (0,))
        load_bytes(0, (0,), (1,))
        load_bytes(0, (1,))
        load_recon(1)
        load_bytes(1)
        load_recon(2)
        load_recon(3)
        nc.sync.dma_start(out=weight[:], in_=frame_weight.rearrange("(g p t) -> p g t", p=P, t=J))
        load_bytes(2)
        load_bytes(3)
        load_commands(0)
        load_bytes(4)
        load_bytes(5)
        load_commands(1)
        load_bytes(6)
        load_bytes(7)

        nc.scalar.activation(out=warm[:], in_=warm[:], func=TANH)
        turn_scales()
        interleave_recon(0, vector_copy)
        for bank_index in range(3):
            spread_scales(bank_index, scalar_copy)
        nc.scalar.copy(out=gain_rows32[:], in_=gain_rows[:])

        stage1_blocks = stage1_steps()
        h_blocks = {}
        for step, blocks in stage1_blocks.items():
            for unit, mb in blocks:
                if unit % 2 == 1:
                    h_blocks.setdefault(step + 1, []).append((unit // 2, mb))

        for step in range(STEPS):
            if step >= 1:
                group_slopes(step - 1, (scalar_copy, scalar_copy))
            for g, mb in h_blocks.get(step, []):
                turn_h(g, mb, "hturn%d" % (mb % 2))
            for piece, piece_step in enumerate(COMMAND_STEPS):
                if piece_step == step:
                    interleave_commands(piece)

            blocks = stage1_blocks.get(step, [])
            before = len(blocks) // 2
            for unit, mb in blocks[:before]:
                stage1(unit, mb, "acc%d" % (mb % 2))
                limit(unit, mb)
            if step in OPEN_STEPS:
                g = OPEN_STEPS[step]
                for half in range(2):
                    stage2(0, half, (g,), "resp%d" % half if g == 0 else None)
            for mb, half in PARTIAL_STEPS.get(step, ()):
                stage2(mb, half, (0, 1), "hturn%d" % ((mb + half) % 2), last=1)
                keep_partial(mb, half)
            if step < PASSES - 1:
                interleave_recon(step + 1, scalar_copy)

            widen(step)
            if step == 0:
                spread_scales(3, vector_copy)
            turn_slopes(step, 0)
            for unit, mb in blocks[before:]:
                stage1(unit, mb, "acc%d" % (mb % 2))
                limit(unit, mb)
            turn_slopes(step, 1)

            for g, mb in h_blocks.get(step, []):
                weigh_h(g, mb)
            if step >= 1:
                quantize_slopes(step - 1)
            if step < PASSES:
                quantize_recon(step)
            for block in range(COMMAND_BLOCKS_IN_STEPS):
                if COMMAND_STEPS[2 * block + 1] == step - 1:
                    quantize_commands(block)
            for g, mb in h_blocks.get(step, []):
                if mb == MODE_BLOCKS - 1:
                    quantize_h(g, 0, MODE_BLOCKS)

            if step == 2:
                gain_bank = psum.tile([P, P], F32, name="hturn0")
                nc.tensor.transpose(gain_bank[:], gain_rows32[:], ident[:])
            if step == 3:
                nc.vector.tensor_copy(out=gain_cols[:], in_=gain_bank[:, 0:MODE_BLOCKS])
            for g in (0, 1):
                if step == COMMAND_STEPS[4 * g + 3]:
                    load_commands(g + 2)

        group_slopes(STEPS - 1, (scalar_copy, vector_copy))
        quantize_slopes(STEPS - 1)
        stage2(0, 0, (2,))
        stage2(1, 0, (0, 1, 2), "hturn0")
        for mb in range(3):
            stage1(LAST, mb, "acc%d" % (mb % 2))
            limit(LAST, mb)
        for block in (6, 5, 7):
            quantize_commands(block)
        turn_h(3, 0, "turn0")
        turn_h(3, 1, "turn1")
        stage1(LAST, 3, "acc1")
        limit(LAST, 3)
        turn_h(3, 2, "acc0")
        weigh_h(3, 0)

        weigh_h(3, 1)
        quantize_h(3, 0, 1)
        stage2(0, 0, (3,))
        stage2(0, 1, (2, 3))
        turn_h(3, 3, "acc1")

        weigh_h(3, 2)
        quantize_h(3, 1, 1)
        stage2(1, 1, (0, 1, 2), "hturn1")
        for half in range(2):
            stage2(1, half, (3,))

        weigh_h(3, 3)
        quantize_h(3, 2, 1)
        for half in range(2):
            stage2(2, half, (2, 3), "turn%d" % half)

        quantize_h(3, 3, 1)
        for half in range(2):
            stage2(3, half, (2, 3), "acc%d" % half)

        for mb in range(MODE_BLOCKS):
            for half in range(2):
                store(mb, half)
